import numpy as np
import ml_dtypes


def mxq(x, axis, fmt="e4m3"):
    dtype, down = {"e4m3": (ml_dtypes.float8_e4m3fn, 7), "e5m2": (ml_dtypes.float8_e5m2, 14)}[fmt]
    v = np.moveaxis(np.asarray(x, np.float32).astype(ml_dtypes.bfloat16).astype(np.float64), axis, -1)
    blocks = v.reshape(v.shape[:-1] + (-1, 32))
    amax = np.abs(blocks).max(-1, keepdims=True)
    byte = np.maximum(np.where(amax > 0, np.frexp(amax)[1] - 1 + 127, 0) - down, 1)
    scale = np.exp2(byte - 127.0)
    codes = (blocks / scale).astype(np.float32).astype(dtype).astype(np.float64)
    return np.moveaxis((codes * scale).reshape(v.shape), -1, axis)


WIDE = False


def mx_kscale(k):
    if not WIDE:
        return np.ones(k)
    levels = np.array([30, -30])
    if k % 512:
        return np.exp2(np.random.permutation(np.resize(levels, k // 32))).repeat(32)
    a = np.empty((k // 512, 16))
    for p in range(k // 512):
        a[p, :8] = np.random.permutation(np.resize(levels, 8))
        for g in range(8):
            far = levels[np.abs(levels - a[p, g]) >= 10]
            a[p, g + 8] = far[np.random.randint(len(far))]
    return np.exp2(a.ravel()).repeat(32)


BF16 = ml_dtypes.bfloat16


def bf(x):
    return np.asarray(x, np.float32).astype(BF16)


def f64(x):
    return np.asarray(x).astype(np.float64)


M, L, D, N = 2048, 1024, 1024, 512


def setup_inputs():
    s, u, v = mx_kscale(D), mx_kscale(M), mx_kscale(L)
    x = np.random.standard_normal((M, D))
    centres = 0.5 * np.random.standard_normal((N, D)) / np.sqrt(D)
    resp = np.exp(np.random.standard_normal((M, N)) - 1.0) / np.sqrt(M)
    labels = np.abs(np.random.standard_normal((L, N))) / np.sqrt(L)
    anchors = np.random.standard_normal((L, D))
    return {"x": bf(x * s * u[:, None]),
            "tau": bf((1 + 0.1 * np.random.standard_normal(M)) / u),
            "centres": bf(centres / s),
            "prior": bf(0.3 * np.random.standard_normal(N)),
            "resp": bf(resp / u[:, None]),
            "labels": bf(labels * v[:, None]),
            "anchors": bf(anchors * s / v[:, None]),
            "gain": bf((1 + 0.1 * np.random.standard_normal(D)) / s)}


def reference(x, tau, centres, prior, resp, labels, anchors, gain):
    dots = mxq(f64(x), 1, "e4m3") @ mxq(f64(centres), 1, "e4m3").T
    scores = np.exp(dots * f64(tau)[:, None] + f64(prior))
    fixed = mxq(f64(labels), 0, "e4m3").T @ mxq(f64(anchors), 0, "e4m3")
    soft = mxq(f64(resp), 0, "e5m2").T @ mxq(f64(x), 0, "e4m3")
    new_centres = (fixed + soft) * f64(gain)
    return scores, new_centres

@@ -1,0 +1,236 @@
+from contextlib import ExitStack
+
+import concourse.mybir as mybir
+from concourse.masks import make_identity
+
+M, L, D, N = 2048, 1024, 1024, 512
+FLOPS = 2 * M * D * N + 2 * L * N * D + 2 * M * N * D
+
+F32 = mybir.dt.float32
+BF16 = mybir.dt.bfloat16
+U32 = mybir.dt.uint32
+U8 = mybir.dt.uint8
+E4M3 = mybir.dt.float8_e4m3fn_x4
+E5M2 = mybir.dt.float8_e5m2_x4
+ALU = mybir.AluOpType
+ACT = mybir.ActivationFunctionType
+
+P = 128
+PACK = 4
+K_PASS = P * PACK
+W = 512
+VC_HEAD = 304
+VC_MAIN = 304
+VC_TAIL = 240
+RUN = 4
+LOADS = ["x0", "cen", "r0", "x1", "r1", "x2", "r2", "x3", "r3", "l0", "a0", "l1", "a1"]
+UNITS = ["x0a", "x0b", "r0a", "x1a", "r1a", "x2a", "r2a", "x3a", "r3a", "l0a", "a0a", "l1a", "a1a", "x1b", "x2b", "x3b", "a0b", "a1b"]
+PAIRS = [2, 3, 0, 1, 4, 5, 6, 7, 8, 9]
+SPLIT = ["x0"]
+FIRST = 2
+GA = [-3, -2, 0, 1]
+MAXP = 1
+K1 = 11
+
+
+def tile_soft_cluster_step_s2_kernel(tc, x, tau, centres, prior, resp, labels, anchors, gain, out_0, out_1):
+    nc = tc.nc
+    with ExitStack() as ctx:
+        keep = ctx.enter_context(tc.tile_pool(name="keep", bufs=1))
+        stage = ctx.enter_context(tc.tile_pool(name="stage", bufs=4))
+        psum = ctx.enter_context(tc.psum_pool(name="psum", bufs=1))
+        ctx.enter_context(tc.manual_schedule())
+
+        warm = keep.tile([P, 1], F32, name="warm")
+        nc.vector.memset(warm[:], 0.0)
+        nc.scalar.activation(out=warm[:], in_=warm[:], func=ACT.Exp)
+        ident = keep.tile([P, P], F32, name="ident")
+        make_identity(nc, ident[:])
+
+        source = {"x": x, "r": resp, "l": labels, "a": anchors}
+        raw = {}
+
+        def load(key):
+            if key == "cen":
+                t = keep.tile([P, PACK, D], BF16, name="raw_cen")
+                nc.sync.dma_start(out=t[:], in_=centres.rearrange("(j p) d -> p j d", p=P))
+                raw["cena"], raw["cenb"] = t[:, :, :W], t[:, :, W:]
+                return
+            g = int(key[1])
+            rows = source[key[0]][g * K_PASS:(g + 1) * K_PASS, :].rearrange("(p j) w -> p j w", j=PACK)
+            if key in SPLIT:
+                for half, c0 in (("a", 0), ("b", W)):
+                    t = keep.tile([P, PACK, W], BF16, name="raw_" + key + half)
+                    nc.sync.dma_start(out=t[:], in_=rows[:, :, c0:c0 + W])
+                    raw[key + half] = t[:]
+            else:
+                t = keep.tile([P, PACK, rows.shape[2]], BF16, name="raw_" + key)
+                nc.sync.dma_start(out=t[:], in_=rows)
+                raw[key + "a"] = t[:, :, :W]
+                raw[key + "b"] = t[:, :, W:]
+
+        prior_rows = keep.tile([P, N // P], BF16, name="prior_rows")
+        nc.sync.dma_start(out=prior_rows[:], in_=prior.rearrange("(p j) -> p j", p=P))
+        gain_rows = keep.tile([P, D // P], BF16, name="gain_rows")
+        nc.sync.dma_start(out=gain_rows[:], in_=gain.rearrange("(p j) -> p j", p=P))
+        load(LOADS[0])
+        load(LOADS[1])
+        tau_sb = keep.tile([P, M // K_PASS, PACK], BF16, name="tau_sb")
+        nc.sync.dma_start(out=tau_sb[:], in_=tau.rearrange("(g p j) -> p g j", p=P, j=PACK))
+        for key in LOADS[2:]:
+            load(key)
+
+        def spread(rows, name):
+            words = rows[:].bitcast(F32)
+            n = words.shape[1]
+            bank = psum.tile([P, n, P], F32, name="spread_" + name, tag="work", bufs=4)
+            for w in range(n):
+                nc.tensor.transpose(bank[:, w, :], words[:, w:w + 1].to_broadcast([P, P]), ident[:])
+            wide = keep.tile([P, 2 * n * P], BF16, name=name)
+            nc.scalar.copy(out=wide[:].bitcast(F32).rearrange("p (r w) -> p r w", w=n), in_=bank[:].rearrange("p w r -> p r w"))
+            return wide
+
+        grouped = {}
+        codes = {}
+        scales = {}
+
+        def interleave(unit):
+            t = stage.tile([P, W, PACK], BF16, name="grp_" + unit, tag="grp", align_bytes=64)
+            grouped[unit] = t
+            vc = VC_HEAD if UNITS.index(unit) < 3 else VC_MAIN if UNITS.index(unit) < K1 else VC_TAIL
+            for engine_copy, lo, hi in ((nc.vector.tensor_copy, 0, vc), (nc.scalar.copy, vc, W)):
+                if lo < hi:
+                  engine_copy(out=t[:, lo:hi, :].rearrange("p (c i) t -> p c t i", i=RUN),
+                            in_=raw[unit][:, :, lo:hi].rearrange("p t (c i) -> p c t i", i=RUN))
+
+        def quantize(unit, fmt):
+            codes[unit] = keep.tile([P, W], U32, name="codes_" + unit, align_bytes=64)
+            scales[unit] = keep.tile([P, W], U8, name="scales_" + unit, align_bytes=64)
+            nc.vector.quantize_mx(out=codes[unit][:].bitcast(fmt), scales=scales[unit][:],
+                                  in_=grouped[unit][:].rearrange("p c t -> p (c t)"))
+
+        def fmt_of(unit):
+            return E5M2 if unit[0] == "r" else E4M3
+
+        banks = {}
+
+        def transposes(q):
+            for b in range(2):
+                bank = psum.tile([P, 2, 2, P], F32, name="tr_%d_%d" % (q, b), tag="work", bufs=4)
+                banks[q, b] = bank
+                for s in range(2):
+                    if q < 2:
+                        key, j, h = "cen", 2 * b + s, q
+                    else:
+                        key, j, h = "x%d" % ((q - 2) // 2), 2 * (q % 2) + b, s
+                    words = raw[key + "ab"[h]][:, j, :].bitcast(F32)
+                    for u in range(2):
+                        nc.tensor.transpose(bank[:, s, u, :], words[:, u::2], ident[:])
+
+        def evacuate(q, b):
+            unit = "t%d" % q
+            if b == 0:
+                grouped[unit] = stage.tile([P, W, PACK], BF16, name="grp_" + unit, tag="tgrp", bufs=2, align_bytes=64)
+            words = grouped[unit][:].rearrange("p c t -> p (c t)").bitcast(F32)
+            nc.scalar.copy(out=words[:, b * W:(b + 1) * W].rearrange("p (s r u) -> p s r u", s=2, u=2),
+                           in_=banks[q, b][:].rearrange("p s u r -> p s r u"))
+
+        dots = {}
+        logits = {}
+
+        def dot(i):
+            unit = "t%d" % (2 + i // 2)
+            dots[i] = psum.tile([P, N], F32, name="dots_%d" % i, tag="work", bufs=4)
+            for h in range(2):
+                cols = slice((2 * (i % 2) + h) * P, (2 * (i % 2) + h + 1) * P)
+                nc.tensor.matmul_mx(out=dots[i][:], lhsT=codes[unit][:, cols].bitcast(E4M3), lhsT_scale=scales[unit][:, cols],
+                                    rhs=codes["t%d" % h][:].bitcast(E4M3), rhs_scale=scales["t%d" % h][:],
+                                    start=(h == 0), stop=(h == 1))
+
+        def logit(i):
+            logits[i] = stage.tile([P, N], F32, name="logit_%d" % i, tag="logit", bufs=16)
+            nc.vector.scalar_tensor_tensor(out=logits[i][:], in0=dots[i][:], scalar=tau_sb[:, i // 4, i % 4:i % 4 + 1],
+                                           in1=prior_wide[:], op0=ALU.mult, op1=ALU.add)
+
+        score_rows = out_0.rearrange("(g p j) c -> g j p c", p=P, j=PACK)
+
+        def score(i):
+            nc.scalar.activation(out=logits[i][:], in_=logits[i][:], func=ACT.Exp)
+            nc.sync.dma_start(out=score_rows[i // 4, i % 4], in_=logits[i][:])
+
+        partner = {"x": "r", "a": "l"}
+        acc = {}
+        issued = {"a": [], "b": []}
+
+        def centre_passes(half, ready):
+            todo = [u for u in UNITS if u[2] == half and u[0] in partner and u in ready
+                    and partner[u[0]] + u[1] + "a" in ready and u not in issued[half]]
+            for u in todo:
+                weights = partner[u[0]] + u[1] + "a"
+                first = len(issued[half]) == 0
+                issued[half].append(u)
+                last = len(issued[half]) == 6
+                for ct in range(4):
+                    if first:
+                        acc[half, ct] = psum.tile([P, W], F32, name="acc_%s%d" % (half, ct), tag="acc" if half == "a" else "work", bufs=4)
+                    cols = slice(ct * P, (ct + 1) * P)
+                    nc.tensor.matmul_mx(out=acc[half, ct][:], lhsT=codes[weights][:, cols].bitcast(fmt_of(weights)),
+                                        lhsT_scale=scales[weights][:, cols], rhs=codes[u][:].bitcast(E4M3), rhs_scale=scales[u][:],
+                                        start=first, stop=last)
+                if todo.index(u) + 1 == MAXP:
+                    return
+
+        def centre_out(half, ct):
+            c0 = W if half == "b" else 0
+            t = stage.tile([P, W], F32, name="new_%s%d" % (half, ct), tag="new", bufs=8)
+            nc.vector.tensor_tensor(out=t[:], in0=acc[half, ct][:], in1=gain_wide[:, c0:c0 + W], op=ALU.mult)
+            nc.sync.dma_start(out=out_1[ct * P:(ct + 1) * P, c0:c0 + W], in_=t[:])
+
+        prior_wide = spread(prior_rows, "prior_wide")
+        gain_wide = spread(gain_rows, "gain_wide")
+
+        ready = []
+
+        def quantize_unit(unit):
+            quantize(unit, fmt_of(unit))
+            ready.append(unit)
+
+        interleave(UNITS[0])
+        interleave(UNITS[1])
+        quantize_unit(UNITS[0])
+        tiles = {r: [2 * (r - 5), 2 * (r - 5) + 1] for r in range(5, 13)}
+        units = {FIRST + k: u for k, u in enumerate(UNITS[2:13])}
+        for r in range(14):
+            if r < 10:
+                transposes(PAIRS[r])
+            centre_passes("a", ready)
+            if r in units:
+                interleave(units[r])
+            if r == 0:
+                quantize_unit(UNITS[1])
+            if r < 10:
+                evacuate(PAIRS[r], 0)
+                evacuate(PAIRS[r], 1)
+            for i in tiles.get(r, []):
+                logit(i)
+            for i in tiles.get(r, []):
+                score(i)
+            if 1 <= r <= 10:
+                quantize("t%d" % PAIRS[r - 1], E4M3)
+            for i in tiles.get(r + 1, []):
+                dot(i)
+            if r in units:
+                quantize_unit(units[r])
+        tail = UNITS[13:]
+        for s in range(len(tail) + 2):
+            centre_passes("a", ready)
+            centre_passes("b", ready)
+            if s < len(tail):
+                interleave(tail[s])
+            for ct in range(4):
+                if s == len(tail) - 1 + GA[ct]:
+                    centre_out("a", ct)
+            if 1 <= s <= len(tail):
+                quantize_unit(tail[s - 1])
+        for ct in range(4):
+            centre_out("b", ct)

@@ -19,18 +19,37 @@ P = 128
 PACK = 4
 K_PASS = P * PACK
 W = 512
-VC_HEAD = 304
-VC_MAIN = 304
-VC_TAIL = 240
+VC_HEAD = 352
+VC_MAIN = 160
+VC_TAIL = 192
 RUN = 4
 LOADS = ["x0", "cen", "r0", "x1", "r1", "x2", "r2", "x3", "r3", "l0", "a0", "l1", "a1"]
 UNITS = ["x0a", "x0b", "r0a", "x1a", "r1a", "x2a", "r2a", "x3a", "r3a", "l0a", "a0a", "l1a", "a1a", "x1b", "x2b", "x3b", "a0b", "a1b"]
 PAIRS = [2, 3, 0, 1, 4, 5, 6, 7, 8, 9]
-SPLIT = ["x0"]
+SPLIT = ["x0", "cen", "x1"]
 FIRST = 2
-GA = [-3, -2, 0, 1]
-MAXP = 1
+GA = [16, 17, 18, 20]
+MAXP = 2
 K1 = 11
+HOLD = 0
+TD = [3, 4, 5, 5]
+VC_LAST = 192
+K2 = 16
+QL = 2
+G0 = 6
+G1 = 14
+GC_MAIN = 160
+GC_TAIL = 0
+D0 = 6
+D1 = 10
+QH = 5
+VF = 4
+KH = 6
+TL = 1
+
+
+def SM(nc):
+    return nc.scalar
 
 
 def tile_soft_cluster_step_s2_kernel(tc, x, tau, centres, prior, resp, labels, anchors, gain, out_0, out_1):
@@ -41,9 +60,6 @@ def tile_soft_cluster_step_s2_kernel(tc, x, tau, centres, prior, resp, labels, a
         psum = ctx.enter_context(tc.psum_pool(name="psum", bufs=1))
         ctx.enter_context(tc.manual_schedule())
 
-        warm = keep.tile([P, 1], F32, name="warm")
-        nc.vector.memset(warm[:], 0.0)
-        nc.scalar.activation(out=warm[:], in_=warm[:], func=ACT.Exp)
         ident = keep.tile([P, P], F32, name="ident")
         make_identity(nc, ident[:])
 
@@ -52,12 +68,10 @@ def tile_soft_cluster_step_s2_kernel(tc, x, tau, centres, prior, resp, labels, a
 
         def load(key):
             if key == "cen":
-                t = keep.tile([P, PACK, D], BF16, name="raw_cen")
-                nc.sync.dma_start(out=t[:], in_=centres.rearrange("(j p) d -> p j d", p=P))
-                raw["cena"], raw["cenb"] = t[:, :, :W], t[:, :, W:]
-                return
-            g = int(key[1])
-            rows = source[key[0]][g * K_PASS:(g + 1) * K_PASS, :].rearrange("(p j) w -> p j w", j=PACK)
+                rows = centres.rearrange("(j p) d -> p j d", p=P)
+            else:
+                g = int(key[1])
+                rows = source[key[0]][g * K_PASS:(g + 1) * K_PASS, :].rearrange("(p j) w -> p j w", j=PACK)
             if key in SPLIT:
                 for half, c0 in (("a", 0), ("b", W)):
                     t = keep.tile([P, PACK, W], BF16, name="raw_" + key + half)
@@ -70,15 +84,18 @@ def tile_soft_cluster_step_s2_kernel(tc, x, tau, centres, prior, resp, labels, a
                 raw[key + "b"] = t[:, :, W:]
 
         prior_rows = keep.tile([P, N // P], BF16, name="prior_rows")
-        nc.sync.dma_start(out=prior_rows[:], in_=prior.rearrange("(p j) -> p j", p=P))
-        gain_rows = keep.tile([P, D // P], BF16, name="gain_rows")
-        nc.sync.dma_start(out=gain_rows[:], in_=gain.rearrange("(p j) -> p j", p=P))
+        SM(nc).dma_start(out=prior_rows[:], in_=prior.rearrange("(p j) -> p j", p=P))
         load(LOADS[0])
         load(LOADS[1])
         tau_sb = keep.tile([P, M // K_PASS, PACK], BF16, name="tau_sb")
-        nc.sync.dma_start(out=tau_sb[:], in_=tau.rearrange("(g p j) -> p g j", p=P, j=PACK))
+        SM(nc).dma_start(out=tau_sb[:], in_=tau.rearrange("(g p j) -> p g j", p=P, j=PACK))
+        warm = keep.tile([P, 1], F32, name="warm")
+        nc.vector.memset(warm[:], 0.0)
+        nc.scalar.activation(out=warm[:], in_=warm[:], func=ACT.Exp)
         for key in LOADS[2:]:
             load(key)
+        gain_wide = keep.tile([P, D], BF16, name="gain_wide")
+        nc.sync.dma_start(out=gain_wide[:], in_=gain.partition_broadcast(P))
 
         def spread(rows, name):
             words = rows[:].bitcast(F32)
@@ -94,14 +111,24 @@ def tile_soft_cluster_step_s2_kernel(tc, x, tau, centres, prior, resp, labels, a
         codes = {}
         scales = {}
 
-        def interleave(unit):
-            t = stage.tile([P, W, PACK], BF16, name="grp_" + unit, tag="grp", align_bytes=64)
-            grouped[unit] = t
-            vc = VC_HEAD if UNITS.index(unit) < 3 else VC_MAIN if UNITS.index(unit) < K1 else VC_TAIL
-            for engine_copy, lo, hi in ((nc.vector.tensor_copy, 0, vc), (nc.scalar.copy, vc, W)):
-                if lo < hi:
-                  engine_copy(out=t[:, lo:hi, :].rearrange("p (c i) t -> p c t i", i=RUN),
-                            in_=raw[unit][:, :, lo:hi].rearrange("p t (c i) -> p c t i", i=RUN))
+        def interleave(unit, who):
+            k = UNITS.index(unit)
+            if unit not in grouped:
+                grouped[unit] = stage.tile([P, W, PACK], BF16, name="grp_" + unit, tag="grp", bufs=QL + 1, align_bytes=64)
+            t = grouped[unit]
+            gc = 0 if k < G0 else GC_MAIN if k < G1 else GC_TAIL
+            vc = VC_HEAD if k < KH else VC_MAIN if k < K1 else VC_TAIL if k < K2 else VC_LAST
+            lo, hi = {"g": (0, gc), "v": (gc, gc + vc), "s": (gc + vc, W)}[who]
+            if lo == hi:
+                return
+            out = t[:, lo:hi, :].rearrange("p (c i) t -> p c t i", i=RUN)
+            in_ = raw[unit][:, :, lo:hi].rearrange("p t (c i) -> p c t i", i=RUN)
+            if who == "g":
+                nc.gpsimd.tensor_scalar(out=out, in0=in_, scalar1=1.0, scalar2=0.0, op0=ALU.mult, op1=ALU.add)
+            elif who == "v":
+                nc.vector.tensor_copy(out=out, in_=in_)
+            else:
+                nc.scalar.copy(out=out, in_=in_)
 
         def quantize(unit, fmt):
             codes[unit] = keep.tile([P, W], U32, name="codes_" + unit, align_bytes=64)
@@ -140,7 +167,7 @@ def tile_soft_cluster_step_s2_kernel(tc, x, tau, centres, prior, resp, labels, a
 
         def dot(i):
             unit = "t%d" % (2 + i // 2)
-            dots[i] = psum.tile([P, N], F32, name="dots_%d" % i, tag="work", bufs=4)
+            dots[i] = psum.tile([P, N], F32, name="dots_%d" % i, tag="work" if i < 16 - HOLD else "acc", bufs=4)
             for h in range(2):
                 cols = slice((2 * (i % 2) + h) * P, (2 * (i % 2) + h + 1) * P)
                 nc.tensor.matmul_mx(out=dots[i][:], lhsT=codes[unit][:, cols].bitcast(E4M3), lhsT_scale=scales[unit][:, cols],
@@ -187,7 +214,6 @@ def tile_soft_cluster_step_s2_kernel(tc, x, tau, centres, prior, resp, labels, a
             nc.sync.dma_start(out=out_1[ct * P:(ct + 1) * P, c0:c0 + W], in_=t[:])
 
         prior_wide = spread(prior_rows, "prior_wide")
-        gain_wide = spread(gain_rows, "gain_wide")
 
         ready = []
 
@@ -195,19 +221,29 @@ def tile_soft_cluster_step_s2_kernel(tc, x, tau, centres, prior, resp, labels, a
             quantize(unit, fmt_of(unit))
             ready.append(unit)
 
-        interleave(UNITS[0])
-        interleave(UNITS[1])
-        quantize_unit(UNITS[0])
+        for unit in UNITS[:2]:
+            interleave(unit, "v")
+            interleave(unit, "s")
         tiles = {r: [2 * (r - 5), 2 * (r - 5) + 1] for r in range(5, 13)}
-        units = {FIRST + k: u for k, u in enumerate(UNITS[2:13])}
-        for r in range(14):
+        n = len(UNITS)
+        for r in range(n + QL + 1):
             if r < 10:
                 transposes(PAIRS[r])
-            centre_passes("a", ready)
-            if r in units:
-                interleave(units[r])
-            if r == 0:
-                quantize_unit(UNITS[1])
+            if r < D0 or r >= D1:
+                centre_passes("a", ready)
+            if r > max(tiles):
+                centre_passes("b", ready)
+            if 2 <= r < VF:
+                interleave(UNITS[r], "v")
+            if r < 2:
+                quantize_unit(UNITS[r])
+            for k in range(2, n):
+                if r == k + (QL if k >= QH else 1):
+                    quantize_unit(UNITS[k])
+            if 2 <= r + 1 < n:
+                interleave(UNITS[r + 1], "g")
+            if 2 <= r < n:
+                interleave(UNITS[r], "s")
             if r < 10:
                 evacuate(PAIRS[r], 0)
                 evacuate(PAIRS[r], 1)
@@ -215,22 +251,16 @@ def tile_soft_cluster_step_s2_kernel(tc, x, tau, centres, prior, resp, labels, a
                 logit(i)
             for i in tiles.get(r, []):
                 score(i)
+            for ct in range(4):
+                if r == GA[ct]:
+                    assert len(issued["a"]) == 6
+                    centre_out("a", ct)
             if 1 <= r <= 10:
                 quantize("t%d" % PAIRS[r - 1], E4M3)
             for i in tiles.get(r + 1, []):
                 dot(i)
-            if r in units:
-                quantize_unit(units[r])
-        tail = UNITS[13:]
-        for s in range(len(tail) + 2):
-            centre_passes("a", ready)
-            centre_passes("b", ready)
-            if s < len(tail):
-                interleave(tail[s])
-            for ct in range(4):
-                if s == len(tail) - 1 + GA[ct]:
-                    centre_out("a", ct)
-            if 1 <= s <= len(tail):
-                quantize_unit(tail[s - 1])
+            if max(2, VF) <= r < n:
+                interleave(UNITS[r], "v")
+        assert len(issued["b"]) == 6
         for ct in range(4):
             centre_out("b", ct)

@@ -13,254 +13,234 @@ U8 = mybir.dt.uint8
 E4M3 = mybir.dt.float8_e4m3fn_x4
 E5M2 = mybir.dt.float8_e5m2_x4
 ALU = mybir.AluOpType
-ACT = mybir.ActivationFunctionType
 
 P = 128
 PACK = 4
 K_PASS = P * PACK
 W = 512
-VC_HEAD = 352
-VC_MAIN = 160
-VC_TAIL = 192
 RUN = 4
-LOADS = ["x0", "cen", "r0", "x1", "r1", "x2", "r2", "x3", "r3", "l0", "a0", "l1", "a1"]
-UNITS = ["x0a", "x0b", "r0a", "x1a", "r1a", "x2a", "r2a", "x3a", "r3a", "l0a", "a0a", "l1a", "a1a", "x1b", "x2b", "x3b", "a0b", "a1b"]
-PAIRS = [2, 3, 0, 1, 4, 5, 6, 7, 8, 9]
-SPLIT = ["x0", "cen", "x1"]
-FIRST = 2
-GA = [16, 17, 18, 20]
-MAXP = 2
-K1 = 11
-HOLD = 0
-TD = [3, 4, 5, 5]
-VC_LAST = 192
-K2 = 16
-QL = 2
-G0 = 6
-G1 = 14
-GC_MAIN = 160
-GC_TAIL = 0
-D0 = 6
-D1 = 10
-QH = 5
-VF = 4
-KH = 6
-TL = 1
+C_TILES = N // P
+M_TILES = M // P
+
+LOADS = ["x0", "x1", "c0", "r0", "r1", "x2", "r2", "x3", "r3", "l0", "a0", "l1", "a1"]
+
+ROW_SLABS = [("x0", 0), ("x0", 1), ("x1", 0), ("x1", 1), ("r0", 0), ("r1", 0), ("x2", 0), ("r2", 0), ("x3", 0),
+             ("r3", 0), ("l0", 0), ("a0", 0), ("l1", 0), ("a1", 0), ("x2", 1), ("x3", 1), ("a0", 1), ("a1", 1)]
+PARTNER = {"x": "r", "a": "l"}
+
+TURNED_SLABS = [("x0", 0), ("x0", 1), ("x1", 0), ("c0", 0), ("c0", 1),
+                ("x1", 1), ("x2", 0), ("x2", 1), ("x3", 0), ("x3", 1)]
+
+QUANT_LAG = 2
+TILES_A_ROUND = 2
+FIRST_SCORES = TURNED_SLABS.index(("c0", 1)) + 2
+SCORE_ROUNDS = range(FIRST_SCORES, FIRST_SCORES + M_TILES // TILES_A_ROUND)
+
+GPSIMD_COLS = 160
+VECTOR_COLS_HEAD = 352
+VECTOR_COLS_SCORES = 160
+VECTOR_COLS_TAIL = 192
 
 
-def SM(nc):
-    return nc.scalar
+def column_shares(index):
+    if index - 1 in SCORE_ROUNDS:
+        return GPSIMD_COLS, VECTOR_COLS_SCORES
+    return 0, (VECTOR_COLS_HEAD if index <= FIRST_SCORES else VECTOR_COLS_TAIL)
 
 
 def tile_soft_cluster_step_s2_kernel(tc, x, tau, centres, prior, resp, labels, anchors, gain, out_0, out_1):
     nc = tc.nc
     with ExitStack() as ctx:
         keep = ctx.enter_context(tc.tile_pool(name="keep", bufs=1))
-        stage = ctx.enter_context(tc.tile_pool(name="stage", bufs=4))
-        psum = ctx.enter_context(tc.psum_pool(name="psum", bufs=1))
+        stage = ctx.enter_context(tc.tile_pool(name="stage", bufs=1))
+        psum = ctx.enter_context(tc.psum_pool(name="psum", bufs=4))
         ctx.enter_context(tc.manual_schedule())
 
         ident = keep.tile([P, P], F32, name="ident")
         make_identity(nc, ident[:])
 
-        source = {"x": x, "r": resp, "l": labels, "a": anchors}
-        raw = {}
-
-        def load(key):
-            if key == "cen":
-                rows = centres.rearrange("(j p) d -> p j d", p=P)
-            else:
-                g = int(key[1])
-                rows = source[key[0]][g * K_PASS:(g + 1) * K_PASS, :].rearrange("(p j) w -> p j w", j=PACK)
-            if key in SPLIT:
-                for half, c0 in (("a", 0), ("b", W)):
-                    t = keep.tile([P, PACK, W], BF16, name="raw_" + key + half)
-                    nc.sync.dma_start(out=t[:], in_=rows[:, :, c0:c0 + W])
-                    raw[key + half] = t[:]
-            else:
-                t = keep.tile([P, PACK, rows.shape[2]], BF16, name="raw_" + key)
-                nc.sync.dma_start(out=t[:], in_=rows)
-                raw[key + "a"] = t[:, :, :W]
-                raw[key + "b"] = t[:, :, W:]
-
         prior_rows = keep.tile([P, N // P], BF16, name="prior_rows")
-        SM(nc).dma_start(out=prior_rows[:], in_=prior.rearrange("(p j) -> p j", p=P))
-        load(LOADS[0])
-        load(LOADS[1])
-        tau_sb = keep.tile([P, M // K_PASS, PACK], BF16, name="tau_sb")
-        SM(nc).dma_start(out=tau_sb[:], in_=tau.rearrange("(g p j) -> p g j", p=P, j=PACK))
+        nc.scalar.dma_start(out=prior_rows[:], in_=prior.rearrange("(p j) -> p j", p=P))
+        tau_rows = keep.tile([P, M // K_PASS, PACK], BF16, name="tau_rows")
+        nc.scalar.dma_start(out=tau_rows[:], in_=tau.rearrange("(g p j) -> p g j", p=P, j=PACK))
+
         warm = keep.tile([P, 1], F32, name="warm")
         nc.vector.memset(warm[:], 0.0)
-        nc.scalar.activation(out=warm[:], in_=warm[:], func=ACT.Exp)
-        for key in LOADS[2:]:
-            load(key)
+        nc.scalar.activation(out=warm[:], in_=warm[:], func=mybir.ActivationFunctionType.Exp)
+
+        source = {"x": x, "r": resp, "l": labels, "a": anchors}
+        raw = {}
+        for load in LOADS:
+            if load == "c0":
+                rows = centres.rearrange("(j p) d -> p j d", p=P)
+            else:
+                g = int(load[1])
+                rows = source[load[0]][g * K_PASS:(g + 1) * K_PASS, :].rearrange("(p j) w -> p j w", j=PACK)
+            raw[load] = keep.tile([P, PACK, rows.shape[2]], BF16, name="raw_" + load)
+            nc.sync.dma_start(out=raw[load][:], in_=rows)
         gain_wide = keep.tile([P, D], BF16, name="gain_wide")
         nc.sync.dma_start(out=gain_wide[:], in_=gain.partition_broadcast(P))
 
-        def spread(rows, name):
-            words = rows[:].bitcast(F32)
-            n = words.shape[1]
-            bank = psum.tile([P, n, P], F32, name="spread_" + name, tag="work", bufs=4)
-            for w in range(n):
-                nc.tensor.transpose(bank[:, w, :], words[:, w:w + 1].to_broadcast([P, P]), ident[:])
-            wide = keep.tile([P, 2 * n * P], BF16, name=name)
-            nc.scalar.copy(out=wide[:].bitcast(F32).rearrange("p (r w) -> p r w", w=n), in_=bank[:].rearrange("p w r -> p r w"))
-            return wide
+        prior_words = prior_rows[:].bitcast(F32)
+        prior_bank = psum.tile([P, 2, P], F32, name="prior_bank", tag="work")
+        for w in range(2):
+            nc.tensor.transpose(prior_bank[:, w, :], prior_words[:, w:w + 1].to_broadcast([P, P]), ident[:])
+        prior_wide = keep.tile([P, N], BF16, name="prior_wide")
+        nc.scalar.copy(out=prior_wide[:].bitcast(F32).rearrange("p (r w) -> p r w", w=2),
+                       in_=prior_bank[:].rearrange("p w r -> p r w"))
 
-        grouped = {}
-        codes = {}
-        scales = {}
+        def quantize(slab, fmt, name):
+            codes = keep.tile([P, W], U32, name="codes_" + name, align_bytes=64)
+            scales = keep.tile([P, W], U8, name="scales_" + name, align_bytes=64)
+            nc.vector.quantize_mx(out=codes[:].bitcast(fmt), scales=scales[:], in_=slab[:].rearrange("p c t -> p (c t)"))
+            return codes, scales, fmt
 
-        def interleave(unit, who):
-            k = UNITS.index(unit)
-            if unit not in grouped:
-                grouped[unit] = stage.tile([P, W, PACK], BF16, name="grp_" + unit, tag="grp", bufs=QL + 1, align_bytes=64)
-            t = grouped[unit]
-            gc = 0 if k < G0 else GC_MAIN if k < G1 else GC_TAIL
-            vc = VC_HEAD if k < KH else VC_MAIN if k < K1 else VC_TAIL if k < K2 else VC_LAST
-            lo, hi = {"g": (0, gc), "v": (gc, gc + vc), "s": (gc + vc, W)}[who]
-            if lo == hi:
-                return
-            out = t[:, lo:hi, :].rearrange("p (c i) t -> p c t i", i=RUN)
-            in_ = raw[unit][:, :, lo:hi].rearrange("p t (c i) -> p c t i", i=RUN)
-            if who == "g":
+        def mx_pass(bank, stationary, tile, moving, start, stop):
+            cols = slice(tile * P, (tile + 1) * P)
+            nc.tensor.matmul_mx(out=bank[:], lhsT=stationary[0][:, cols].bitcast(stationary[2]),
+                                lhsT_scale=stationary[1][:, cols], rhs=moving[0][:].bitcast(moving[2]),
+                                rhs_scale=moving[1][:], start=start, stop=stop)
+
+        row_slab = {}
+        row_mx = {}
+
+        def new_row_slab(index):
+            row_slab[index] = stage.tile([P, W, PACK], BF16, name="row_slab_%d" % index, tag="row_slab",
+                                         bufs=QUANT_LAG + 1, align_bytes=64)
+
+        def copy_rows(index, engine):
+            load, half = ROW_SLABS[index]
+            g_cols, v_cols = column_shares(index)
+            lo, hi = {"gpsimd": (0, g_cols), "vector": (g_cols, g_cols + v_cols), "scalar": (g_cols + v_cols, W)}[engine]
+            out = row_slab[index][:, lo:hi, :].rearrange("p (c i) t -> p c t i", i=RUN)
+            in_ = raw[load][:, :, half * W + lo:half * W + hi].rearrange("p t (c i) -> p c t i", i=RUN)
+            if engine == "gpsimd":
                 nc.gpsimd.tensor_scalar(out=out, in0=in_, scalar1=1.0, scalar2=0.0, op0=ALU.mult, op1=ALU.add)
-            elif who == "v":
+            elif engine == "vector":
                 nc.vector.tensor_copy(out=out, in_=in_)
             else:
                 nc.scalar.copy(out=out, in_=in_)
 
-        def quantize(unit, fmt):
-            codes[unit] = keep.tile([P, W], U32, name="codes_" + unit, align_bytes=64)
-            scales[unit] = keep.tile([P, W], U8, name="scales_" + unit, align_bytes=64)
-            nc.vector.quantize_mx(out=codes[unit][:].bitcast(fmt), scales=scales[unit][:],
-                                  in_=grouped[unit][:].rearrange("p c t -> p (c t)"))
+        def quantize_rows(index):
+            load, half = ROW_SLABS[index]
+            row_mx[load, half] = quantize(row_slab[index], E5M2 if load[0] == "r" else E4M3, "%s_%d" % (load, half))
 
-        def fmt_of(unit):
-            return E5M2 if unit[0] == "r" else E4M3
+        turned_slab = {}
+        turned_mx = {}
 
-        banks = {}
-
-        def transposes(q):
+        def transposes(load, half):
+            banks = []
             for b in range(2):
-                bank = psum.tile([P, 2, 2, P], F32, name="tr_%d_%d" % (q, b), tag="work", bufs=4)
-                banks[q, b] = bank
+                bank = psum.tile([P, 2, 2, P], F32, name="turn_%s_%d_%d" % (load, half, b), tag="work")
                 for s in range(2):
-                    if q < 2:
-                        key, j, h = "cen", 2 * b + s, q
-                    else:
-                        key, j, h = "x%d" % ((q - 2) // 2), 2 * (q % 2) + b, s
-                    words = raw[key + "ab"[h]][:, j, :].bitcast(F32)
+                    j, features = (2 * b + s, half) if load == "c0" else (2 * half + b, s)
+                    words = raw[load][:, j, features * W:(features + 1) * W].bitcast(F32)
                     for u in range(2):
                         nc.tensor.transpose(bank[:, s, u, :], words[:, u::2], ident[:])
+                banks.append(bank)
+            return banks
 
-        def evacuate(q, b):
-            unit = "t%d" % q
-            if b == 0:
-                grouped[unit] = stage.tile([P, W, PACK], BF16, name="grp_" + unit, tag="tgrp", bufs=2, align_bytes=64)
-            words = grouped[unit][:].rearrange("p c t -> p (c t)").bitcast(F32)
-            nc.scalar.copy(out=words[:, b * W:(b + 1) * W].rearrange("p (s r u) -> p s r u", s=2, u=2),
-                           in_=banks[q, b][:].rearrange("p s u r -> p s r u"))
-
-        dots = {}
-        logits = {}
-
-        def dot(i):
-            unit = "t%d" % (2 + i // 2)
-            dots[i] = psum.tile([P, N], F32, name="dots_%d" % i, tag="work" if i < 16 - HOLD else "acc", bufs=4)
-            for h in range(2):
-                cols = slice((2 * (i % 2) + h) * P, (2 * (i % 2) + h + 1) * P)
-                nc.tensor.matmul_mx(out=dots[i][:], lhsT=codes[unit][:, cols].bitcast(E4M3), lhsT_scale=scales[unit][:, cols],
-                                    rhs=codes["t%d" % h][:].bitcast(E4M3), rhs_scale=scales["t%d" % h][:],
-                                    start=(h == 0), stop=(h == 1))
-
-        def logit(i):
-            logits[i] = stage.tile([P, N], F32, name="logit_%d" % i, tag="logit", bufs=16)
-            nc.vector.scalar_tensor_tensor(out=logits[i][:], in0=dots[i][:], scalar=tau_sb[:, i // 4, i % 4:i % 4 + 1],
-                                           in1=prior_wide[:], op0=ALU.mult, op1=ALU.add)
+        def copy_turned(load, half, banks):
+            slab = stage.tile([P, W, PACK], BF16, name="turned_%s_%d" % (load, half), tag="turned_slab", bufs=2,
+                              align_bytes=64)
+            words = slab[:].rearrange("p c t -> p (c t)").bitcast(F32)
+            for b in range(2):
+                nc.scalar.copy(out=words[:, b * W:(b + 1) * W].rearrange("p (s r u) -> p s r u", s=2, u=2),
+                               in_=banks[b][:].rearrange("p s u r -> p s r u"))
+            turned_slab[load, half] = slab
 
         score_rows = out_0.rearrange("(g p j) c -> g j p c", p=P, j=PACK)
+        dots = {}
+        scores = {}
 
-        def score(i):
-            nc.scalar.activation(out=logits[i][:], in_=logits[i][:], func=ACT.Exp)
-            nc.sync.dma_start(out=score_rows[i // 4, i % 4], in_=logits[i][:])
+        def tiles_of(r):
+            if r not in SCORE_ROUNDS:
+                return []
+            return [TILES_A_ROUND * (r - FIRST_SCORES) + k for k in range(TILES_A_ROUND)]
 
-        partner = {"x": "r", "a": "l"}
-        acc = {}
-        issued = {"a": [], "b": []}
+        def dot(i):
+            g, j = divmod(i, PACK)
+            dots[i] = psum.tile([P, N], F32, name="dots_%d" % i, tag="work")
+            for features in range(2):
+                mx_pass(dots[i], turned_mx["x%d" % g, j // 2], 2 * (j % 2) + features, turned_mx["c0", features],
+                        features == 0, features == 1)
 
-        def centre_passes(half, ready):
-            todo = [u for u in UNITS if u[2] == half and u[0] in partner and u in ready
-                    and partner[u[0]] + u[1] + "a" in ready and u not in issued[half]]
-            for u in todo:
-                weights = partner[u[0]] + u[1] + "a"
-                first = len(issued[half]) == 0
-                issued[half].append(u)
-                last = len(issued[half]) == 6
-                for ct in range(4):
+        def logit(i):
+            g, j = divmod(i, PACK)
+            scores[i] = stage.tile([P, N], F32, name="scores_%d" % i)
+            nc.vector.scalar_tensor_tensor(out=scores[i][:], in0=dots[i][:], scalar=tau_rows[:, g, j:j + 1],
+                                           in1=prior_wide[:], op0=ALU.mult, op1=ALU.add)
+
+        def exp_and_store(i):
+            g, j = divmod(i, PACK)
+            nc.scalar.activation(out=scores[i][:], in_=scores[i][:], func=mybir.ActivationFunctionType.Exp)
+            nc.sync.dma_start(out=score_rows[g, j], in_=scores[i][:])
+
+        sums = {}
+        waiting = {half: [load for load, h in ROW_SLABS if h == half and load[0] in PARTNER] for half in range(2)}
+        n_passes = len(waiting[0])
+        passes_a_round = 2
+
+        def centre_passes(half):
+            ready = [load for load in waiting[half]
+                     if (load, half) in row_mx and (PARTNER[load[0]] + load[1], 0) in row_mx]
+            for load in ready[:passes_a_round]:
+                first = len(waiting[half]) == n_passes
+                waiting[half].remove(load)
+                for ct in range(C_TILES):
                     if first:
-                        acc[half, ct] = psum.tile([P, W], F32, name="acc_%s%d" % (half, ct), tag="acc" if half == "a" else "work", bufs=4)
-                    cols = slice(ct * P, (ct + 1) * P)
-                    nc.tensor.matmul_mx(out=acc[half, ct][:], lhsT=codes[weights][:, cols].bitcast(fmt_of(weights)),
-                                        lhsT_scale=scales[weights][:, cols], rhs=codes[u][:].bitcast(E4M3), rhs_scale=scales[u][:],
-                                        start=first, stop=last)
-                if todo.index(u) + 1 == MAXP:
-                    return
+                        sums[half, ct] = psum.tile([P, W], F32, name="sum_%d_%d" % (half, ct),
+                                                   tag="work" if half else "sum")
+                    mx_pass(sums[half, ct], row_mx[PARTNER[load[0]] + load[1], 0], ct, row_mx[load, half],
+                            first, not waiting[half])
 
-        def centre_out(half, ct):
-            c0 = W if half == "b" else 0
-            t = stage.tile([P, W], F32, name="new_%s%d" % (half, ct), tag="new", bufs=8)
-            nc.vector.tensor_tensor(out=t[:], in0=acc[half, ct][:], in1=gain_wide[:, c0:c0 + W], op=ALU.mult)
-            nc.sync.dma_start(out=out_1[ct * P:(ct + 1) * P, c0:c0 + W], in_=t[:])
+        def gain_and_store(half, ct):
+            cols = slice(half * W, (half + 1) * W)
+            new = stage.tile([P, W], F32, name="new_%d_%d" % (half, ct))
+            nc.vector.tensor_tensor(out=new[:], in0=sums[half, ct][:], in1=gain_wide[:, cols], op=ALU.mult)
+            nc.sync.dma_start(out=out_1[ct * P:(ct + 1) * P, cols], in_=new[:])
 
-        prior_wide = spread(prior_rows, "prior_wide")
-
-        ready = []
-
-        def quantize_unit(unit):
-            quantize(unit, fmt_of(unit))
-            ready.append(unit)
-
-        for unit in UNITS[:2]:
-            interleave(unit, "v")
-            interleave(unit, "s")
-        tiles = {r: [2 * (r - 5), 2 * (r - 5) + 1] for r in range(5, 13)}
-        n = len(UNITS)
-        for r in range(n + QL + 1):
-            if r < 10:
-                transposes(PAIRS[r])
-            if r < D0 or r >= D1:
-                centre_passes("a", ready)
-            if r > max(tiles):
-                centre_passes("b", ready)
-            if 2 <= r < VF:
-                interleave(UNITS[r], "v")
-            if r < 2:
-                quantize_unit(UNITS[r])
-            for k in range(2, n):
-                if r == k + (QL if k >= QH else 1):
-                    quantize_unit(UNITS[k])
-            if 2 <= r + 1 < n:
-                interleave(UNITS[r + 1], "g")
-            if 2 <= r < n:
-                interleave(UNITS[r], "s")
-            if r < 10:
-                evacuate(PAIRS[r], 0)
-                evacuate(PAIRS[r], 1)
-            for i in tiles.get(r, []):
+        n_rows, n_turned = len(ROW_SLABS), len(TURNED_SLABS)
+        ahead = 2
+        for index in range(ahead):
+            new_row_slab(index)
+            copy_rows(index, "vector")
+            copy_rows(index, "scalar")
+        first_gain = ROW_SLABS.index(("a1", 0)) + QUANT_LAG + 2
+        for r in range(n_rows + QUANT_LAG + 1):
+            copies = ahead <= r < n_rows
+            if r < n_turned:
+                banks = transposes(*TURNED_SLABS[r])
+            else:
+                centre_passes(0)
+            if r > SCORE_ROUNDS[-1]:
+                centre_passes(1)
+            if copies and r < FIRST_SCORES:
+                copy_rows(r, "vector")
+            if r < ahead:
+                quantize_rows(r)
+            if ahead <= r - QUANT_LAG < n_rows:
+                quantize_rows(r - QUANT_LAG)
+            if ahead <= r + 1 < n_rows:
+                new_row_slab(r + 1)
+            if r in SCORE_ROUNDS:
+                copy_rows(r + 1, "gpsimd")
+            if copies:
+                copy_rows(r, "scalar")
+            if r < n_turned:
+                copy_turned(*TURNED_SLABS[r], banks)
+            for i in tiles_of(r):
                 logit(i)
-            for i in tiles.get(r, []):
-                score(i)
-            for ct in range(4):
-                if r == GA[ct]:
-                    assert len(issued["a"]) == 6
-                    centre_out("a", ct)
-            if 1 <= r <= 10:
-                quantize("t%d" % PAIRS[r - 1], E4M3)
-            for i in tiles.get(r + 1, []):
+            for i in tiles_of(r):
+                exp_and_store(i)
+            if 0 <= r - first_gain < C_TILES:
+                gain_and_store(0, r - first_gain)
+            if 0 <= r - 1 < n_turned:
+                load, half = TURNED_SLABS[r - 1]
+                turned_mx[load, half] = quantize(turned_slab[load, half], E4M3, "turned_%s_%d" % (load, half))
+            for i in tiles_of(r + 1):
                 dot(i)
-            if max(2, VF) <= r < n:
-                interleave(UNITS[r], "v")
-        assert len(issued["b"]) == 6
-        for ct in range(4):
-            centre_out("b", ct)
+            if copies and r >= FIRST_SCORES:
+                copy_rows(r, "vector")
+        for ct in range(C_TILES):
+            gain_and_store(1, ct)

from contextlib import ExitStack

import concourse.mybir as mybir
from concourse.masks import make_identity

M, L, D, N = 2048, 1024, 1024, 512
FLOPS = 2 * M * D * N + 2 * L * N * D + 2 * M * N * D

F32 = mybir.dt.float32
BF16 = mybir.dt.bfloat16
U32 = mybir.dt.uint32
U8 = mybir.dt.uint8
E4M3 = mybir.dt.float8_e4m3fn_x4
E5M2 = mybir.dt.float8_e5m2_x4
ALU = mybir.AluOpType

P = 128
PACK = 4
K_PASS = P * PACK
W = 512
RUN = 4
C_TILES = N // P
M_TILES = M // P

LOADS = ["x0", "x1", "c0", "r0", "r1", "x2", "r2", "x3", "r3", "l0", "a0", "l1", "a1"]

ROW_SLABS = [("x0", 0), ("x0", 1), ("x1", 0), ("x1", 1), ("r0", 0), ("r1", 0), ("x2", 0), ("r2", 0), ("x3", 0),
             ("r3", 0), ("l0", 0), ("a0", 0), ("l1", 0), ("a1", 0), ("x2", 1), ("x3", 1), ("a0", 1), ("a1", 1)]
PARTNER = {"x": "r", "a": "l"}

TURNED_SLABS = [("x0", 0), ("x0", 1), ("x1", 0), ("c0", 0), ("c0", 1),
                ("x1", 1), ("x2", 0), ("x2", 1), ("x3", 0), ("x3", 1)]

QUANT_LAG = 2
TILES_A_ROUND = 2
FIRST_SCORES = TURNED_SLABS.index(("c0", 1)) + 2
SCORE_ROUNDS = range(FIRST_SCORES, FIRST_SCORES + M_TILES // TILES_A_ROUND)

GPSIMD_COLS = 160
VECTOR_COLS_HEAD = 352
VECTOR_COLS_SCORES = 160
VECTOR_COLS_TAIL = 192


def column_shares(index):
    if index - 1 in SCORE_ROUNDS:
        return GPSIMD_COLS, VECTOR_COLS_SCORES
    return 0, (VECTOR_COLS_HEAD if index <= FIRST_SCORES else VECTOR_COLS_TAIL)


def tile_soft_cluster_step_s2_kernel(tc, x, tau, centres, prior, resp, labels, anchors, gain, out_0, out_1):
    nc = tc.nc
    with ExitStack() as ctx:
        keep = ctx.enter_context(tc.tile_pool(name="keep", bufs=1))
        stage = ctx.enter_context(tc.tile_pool(name="stage", bufs=1))
        psum = ctx.enter_context(tc.psum_pool(name="psum", bufs=4))
        ctx.enter_context(tc.manual_schedule())

        ident = keep.tile([P, P], F32, name="ident")
        make_identity(nc, ident[:])

        prior_rows = keep.tile([P, N // P], BF16, name="prior_rows")
        nc.scalar.dma_start(out=prior_rows[:], in_=prior.rearrange("(p j) -> p j", p=P))
        tau_rows = keep.tile([P, M // K_PASS, PACK], BF16, name="tau_rows")
        nc.scalar.dma_start(out=tau_rows[:], in_=tau.rearrange("(g p j) -> p g j", p=P, j=PACK))

        warm = keep.tile([P, 1], F32, name="warm")
        nc.vector.memset(warm[:], 0.0)
        nc.scalar.activation(out=warm[:], in_=warm[:], func=mybir.ActivationFunctionType.Exp)

        source = {"x": x, "r": resp, "l": labels, "a": anchors}
        raw = {}
        for load in LOADS:
            if load == "c0":
                rows = centres.rearrange("(j p) d -> p j d", p=P)
            else:
                g = int(load[1])
                rows = source[load[0]][g * K_PASS:(g + 1) * K_PASS, :].rearrange("(p j) w -> p j w", j=PACK)
            raw[load] = keep.tile([P, PACK, rows.shape[2]], BF16, name="raw_" + load)
            nc.sync.dma_start(out=raw[load][:], in_=rows)
        gain_wide = keep.tile([P, D], BF16, name="gain_wide")
        nc.sync.dma_start(out=gain_wide[:], in_=gain.partition_broadcast(P))

        prior_words = prior_rows[:].bitcast(F32)
        prior_bank = psum.tile([P, 2, P], F32, name="prior_bank", tag="work")
        for w in range(2):
            nc.tensor.transpose(prior_bank[:, w, :], prior_words[:, w:w + 1].to_broadcast([P, P]), ident[:])
        prior_wide = keep.tile([P, N], BF16, name="prior_wide")
        nc.scalar.copy(out=prior_wide[:].bitcast(F32).rearrange("p (r w) -> p r w", w=2),
                       in_=prior_bank[:].rearrange("p w r -> p r w"))

        def quantize(slab, fmt, name):
            codes = keep.tile([P, W], U32, name="codes_" + name, align_bytes=64)
            scales = keep.tile([P, W], U8, name="scales_" + name, align_bytes=64)
            nc.vector.quantize_mx(out=codes[:].bitcast(fmt), scales=scales[:], in_=slab[:].rearrange("p c t -> p (c t)"))
            return codes, scales, fmt

        def mx_pass(bank, stationary, tile, moving, start, stop):
            cols = slice(tile * P, (tile + 1) * P)
            nc.tensor.matmul_mx(out=bank[:], lhsT=stationary[0][:, cols].bitcast(stationary[2]),
                                lhsT_scale=stationary[1][:, cols], rhs=moving[0][:].bitcast(moving[2]),
                                rhs_scale=moving[1][:], start=start, stop=stop)

        row_slab = {}
        row_mx = {}

        def new_row_slab(index):
            row_slab[index] = stage.tile([P, W, PACK], BF16, name="row_slab_%d" % index, tag="row_slab",
                                         bufs=QUANT_LAG + 1, align_bytes=64)

        def copy_rows(index, engine):
            load, half = ROW_SLABS[index]
            g_cols, v_cols = column_shares(index)
            lo, hi = {"gpsimd": (0, g_cols), "vector": (g_cols, g_cols + v_cols), "scalar": (g_cols + v_cols, W)}[engine]
            out = row_slab[index][:, lo:hi, :].rearrange("p (c i) t -> p c t i", i=RUN)
            in_ = raw[load][:, :, half * W + lo:half * W + hi].rearrange("p t (c i) -> p c t i", i=RUN)
            if engine == "gpsimd":
                nc.gpsimd.tensor_scalar(out=out, in0=in_, scalar1=1.0, scalar2=0.0, op0=ALU.mult, op1=ALU.add)
            elif engine == "vector":
                nc.vector.tensor_copy(out=out, in_=in_)
            else:
                nc.scalar.copy(out=out, in_=in_)

        def quantize_rows(index):
            load, half = ROW_SLABS[index]
            row_mx[load, half] = quantize(row_slab[index], E5M2 if load[0] == "r" else E4M3, "%s_%d" % (load, half))

        turned_slab = {}
        turned_mx = {}

        def transposes(load, half):
            banks = []
            for b in range(2):
                bank = psum.tile([P, 2, 2, P], F32, name="turn_%s_%d_%d" % (load, half, b), tag="work")
                for s in range(2):
                    j, features = (2 * b + s, half) if load == "c0" else (2 * half + b, s)
                    words = raw[load][:, j, features * W:(features + 1) * W].bitcast(F32)
                    for u in range(2):
                        nc.tensor.transpose(bank[:, s, u, :], words[:, u::2], ident[:])
                banks.append(bank)
            return banks

        def copy_turned(load, half, banks):
            slab = stage.tile([P, W, PACK], BF16, name="turned_%s_%d" % (load, half), tag="turned_slab", bufs=2,
                              align_bytes=64)
            words = slab[:].rearrange("p c t -> p (c t)").bitcast(F32)
            for b in range(2):
                nc.scalar.copy(out=words[:, b * W:(b + 1) * W].rearrange("p (s r u) -> p s r u", s=2, u=2),
                               in_=banks[b][:].rearrange("p s u r -> p s r u"))
            turned_slab[load, half] = slab

        score_rows = out_0.rearrange("(g p j) c -> g j p c", p=P, j=PACK)
        dots = {}
        scores = {}

        def tiles_of(r):
            if r not in SCORE_ROUNDS:
                return []
            return [TILES_A_ROUND * (r - FIRST_SCORES) + k for k in range(TILES_A_ROUND)]

        def dot(i):
            g, j = divmod(i, PACK)
            dots[i] = psum.tile([P, N], F32, name="dots_%d" % i, tag="work")
            for features in range(2):
                mx_pass(dots[i], turned_mx["x%d" % g, j // 2], 2 * (j % 2) + features, turned_mx["c0", features],
                        features == 0, features == 1)

        def logit(i):
            g, j = divmod(i, PACK)
            scores[i] = stage.tile([P, N], F32, name="scores_%d" % i)
            nc.vector.scalar_tensor_tensor(out=scores[i][:], in0=dots[i][:], scalar=tau_rows[:, g, j:j + 1],
                                           in1=prior_wide[:], op0=ALU.mult, op1=ALU.add)

        def exp_and_store(i):
            g, j = divmod(i, PACK)
            nc.scalar.activation(out=scores[i][:], in_=scores[i][:], func=mybir.ActivationFunctionType.Exp)
            nc.sync.dma_start(out=score_rows[g, j], in_=scores[i][:])

        sums = {}
        waiting = {half: [load for load, h in ROW_SLABS if h == half and load[0] in PARTNER] for half in range(2)}
        n_passes = len(waiting[0])
        passes_a_round = 2

        def centre_passes(half):
            ready = [load for load in waiting[half]
                     if (load, half) in row_mx and (PARTNER[load[0]] + load[1], 0) in row_mx]
            for load in ready[:passes_a_round]:
                first = len(waiting[half]) == n_passes
                waiting[half].remove(load)
                for ct in range(C_TILES):
                    if first:
                        sums[half, ct] = psum.tile([P, W], F32, name="sum_%d_%d" % (half, ct),
                                                   tag="work" if half else "sum")
                    mx_pass(sums[half, ct], row_mx[PARTNER[load[0]] + load[1], 0], ct, row_mx[load, half],
                            first, not waiting[half])

        def gain_and_store(half, ct):
            cols = slice(half * W, (half + 1) * W)
            new = stage.tile([P, W], F32, name="new_%d_%d" % (half, ct))
            nc.vector.tensor_tensor(out=new[:], in0=sums[half, ct][:], in1=gain_wide[:, cols], op=ALU.mult)
            nc.sync.dma_start(out=out_1[ct * P:(ct + 1) * P, cols], in_=new[:])

        n_rows, n_turned = len(ROW_SLABS), len(TURNED_SLABS)
        ahead = 2
        for index in range(ahead):
            new_row_slab(index)
            copy_rows(index, "vector")
            copy_rows(index, "scalar")
        first_gain = ROW_SLABS.index(("a1", 0)) + QUANT_LAG + 2
        for r in range(n_rows + QUANT_LAG + 1):
            copies = ahead <= r < n_rows
            if r < n_turned:
                banks = transposes(*TURNED_SLABS[r])
            else:
                centre_passes(0)
            if r > SCORE_ROUNDS[-1]:
                centre_passes(1)
            if copies and r < FIRST_SCORES:
                copy_rows(r, "vector")
            if r < ahead:
                quantize_rows(r)
            if ahead <= r - QUANT_LAG < n_rows:
                quantize_rows(r - QUANT_LAG)
            if ahead <= r + 1 < n_rows:
                new_row_slab(r + 1)
            if r in SCORE_ROUNDS:
                copy_rows(r + 1, "gpsimd")
            if copies:
                copy_rows(r, "scalar")
            if r < n_turned:
                copy_turned(*TURNED_SLABS[r], banks)
            for i in tiles_of(r):
                logit(i)
            for i in tiles_of(r):
                exp_and_store(i)
            if 0 <= r - first_gain < C_TILES:
                gain_and_store(0, r - first_gain)
            if 0 <= r - 1 < n_turned:
                load, half = TURNED_SLABS[r - 1]
                turned_mx[load, half] = quantize(turned_slab[load, half], E4M3, "turned_%s_%d" % (load, half))
            for i in tiles_of(r + 1):
                dot(i)
            if copies and r >= FIRST_SCORES:
                copy_rows(r, "vector")
        for ct in range(C_TILES):
            gain_and_store(1, ct)
